import numpy as np
import ml_dtypes


def mxq(x, axis, fmt="e4m3"):
    dtype, down = {"e4m3": (ml_dtypes.float8_e4m3fn, 7), "e5m2": (ml_dtypes.float8_e5m2, 14)}[fmt]
    v = np.moveaxis(np.asarray(x, np.float32).astype(ml_dtypes.bfloat16).astype(np.float64), axis, -1)
    blocks = v.reshape(v.shape[:-1] + (-1, 32))
    amax = np.abs(blocks).max(-1, keepdims=True)
    byte = np.maximum(np.where(amax > 0, np.frexp(amax)[1] - 1 + 127, 0) - down, 1)
    scale = np.exp2(byte - 127.0)
    codes = (blocks / scale).astype(np.float32).astype(dtype).astype(np.float64)
    return np.moveaxis((codes * scale).reshape(v.shape), -1, axis)


WIDE = False


def mx_kscale(k):
    if not WIDE:
        return np.ones(k)
    levels = np.array([10, -10, 5, -5, 0])
    if k % 512:
        return np.exp2(np.random.permutation(np.resize(levels, k // 32))).repeat(32)
    a = np.empty((k // 512, 16))
    for p in range(k // 512):
        a[p, :8] = np.random.permutation(np.resize(levels, 8))
        for g in range(8):
            far = levels[np.abs(levels - a[p, g]) >= 10]
            a[p, g + 8] = far[np.random.randint(len(far))]
    return np.exp2(a.ravel()).repeat(32)


def f64(x):
    return np.asarray(x).astype(np.float64)


def striped(idx):
    return np.tile(np.asarray(idx).reshape(-1, 16).T, (8, 1)).astype(np.uint16)


def unstriped(offs):
    return offs[:16].T.reshape(-1).astype(np.int64)


D, T, I, Q = 512, 2048, 512, 256


def setup_inputs():
    n = np.random.standard_normal
    idx = np.random.permutation(T)[:I]
    fd = mx_kscale(D)
    return {
        "query": (n((D, Q)) * 0.8 / np.sqrt(D) * fd[:, None]).astype(np.float32),
        "keys": (n((D, T)) * np.random.uniform(0.4, 2.0, (1, T))).astype(np.float32),
        "dsc": (np.random.uniform(0.5, 2.0, (1, D)) / fd).astype(np.float32),
        "lim": (np.random.uniform(0.6, 1.2, (I, 1))).astype(np.float32),
        "offs": striped(idx),
    }


def reference(query, keys, dsc, lim, offs):
    idx = unstriped(offs)
    kt = f64(keys)[:, idx].T
    nr = np.sqrt(np.mean(np.square(kt), axis=1, keepdims=True))
    ks = kt * np.minimum(f64(lim) / nr, 1.0) * f64(dsc)
    km = ks.T
    queryq = mxq(f64(query), 0, "e4m3")
    kmq = mxq(km, 0, "e4m3")
    a = queryq.T @ kmq
    p = np.exp(a - np.max(a, axis=1, keepdims=True))
    y = p / np.sum(p, axis=1, keepdims=True) * 512.0
    return y

from contextlib import ExitStack

import concourse.mybir as mybir
from concourse.masks import make_identity

D, T, I, Q = 512, 2048, 512, 256
FLOPS = 2 * D * I * Q

F32 = mybir.dt.float32
BF16 = mybir.dt.bfloat16
U32 = mybir.dt.uint32
U16 = mybir.dt.uint16
U8 = mybir.dt.uint8
FP8X4 = mybir.dt.float8_e4m3fn_x4
ALU = mybir.AluOpType
ACT = mybir.ActivationFunctionType
AX = mybir.AxisListType

P = 128
PACK = 4
HALF = I // 2
CHUNKS = I // P


def tile_attend_clippedkeys_kernel(tc, query, keys, dsc, lim, offs, out):
    nc = tc.nc
    with ExitStack() as ctx:
        sb = ctx.enter_context(tc.tile_pool(name="sb", bufs=1))
        ps = ctx.enter_context(tc.psum_pool(name="ps", bufs=1))

        offsets = sb.tile([P, I // 16], U16, name="offsets")
        planes = [sb.tile([P, T], F32, name=f"plane{t}") for t in range(PACK)]
        key_rows = keys.rearrange("(p t) w -> p t w", t=PACK)
        lim_rows = sb.tile([P, P], F32, name="lim_rows")
        nc.vector.memset(lim_rows[:], 0.0)
        nc.sync.dma_start(planes[0][:], key_rows[:, 0, :])
        nc.sync.dma_start(offsets[:], offs)
        nc.sync.dma_start(lim_rows[0:CHUNKS, :], lim.rearrange("(c s) o -> c (s o)", s=P))
        for t in range(1, PACK):
            nc.sync.dma_start(planes[t][:], key_rows[:, t, :])
        q_raw = sb.tile([P, PACK, Q], F32, name="q_raw")
        nc.sync.dma_start(q_raw[:], query.rearrange("(p t) q -> p t q", t=PACK))

        one = sb.tile([P, 1], F32, name="one")
        nc.vector.memset(one[:], 1.0)
        warm = sb.tile([P, 1], F32, name="warm")
        nc.scalar.activation(warm[:], one[:], ACT.Sqrt)

        dsc_col = sb.tile([P, PACK], F32, name="dsc_col")
        nc.scalar.dma_start(dsc_col[:], dsc.rearrange("o (p t) -> p (o t)", t=PACK))
        ident = sb.tile([P, P], F32, name="ident")
        make_identity(nc, ident[:])

        first = [ps.tile([P, CHUNKS, P], F32, name=f"first{j}") for j in range(2)]
        second = [ps.tile([P, CHUNKS, P], F32, name=f"second{j}") for j in range(2)]
        banks = [ps.tile([P, PACK, P], F32, name=f"bank{c}") for c in range(CHUNKS)]
        nc.tensor.transpose(second[1][:, 0, :], lim_rows[:], ident[:])
        lim_col = sb.tile([P, CHUNKS], F32, name="lim_col")
        nc.vector.tensor_copy(lim_col[:], second[1][:, 0, 0:CHUNKS])

        root = float(D) ** -0.5
        last = PACK - 1
        junk = sb.tile([P, PACK, CHUNKS, P], F32, name="junk")
        gd = [sb.tile([P, PACK, HALF], F32, name=f"gd{h}") for h in range(2)]
        ms = [[sb.tile([P, 1], F32, name=f"ms{t}_{c}") for c in range(CHUNKS)] for t in range(PACK)]
        run = [[sb.tile([P, 1], F32, name=f"run{t}_{c}") for c in range(CHUNKS)] for t in range(1, PACK)]
        run = [ms[0]] + run
        inv = [sb.tile([P, 1], F32, name=f"inv{c}") for c in range(CHUNKS)]
        fac = [sb.tile([P, 1], F32, name=f"fac{c}") for c in range(CHUNKS)]
        for t in range(PACK):
            g = [sb.tile([P, HALF], F32, name=f"g{t}_{h}") for h in range(2)]
            for h in range(2):
                nc.vector.tensor_copy(g[h][:], planes[t][:].indirect(offsets[:, h * 16:(h + 1) * 16]))
            for c in range(CHUNKS):
                nc.tensor.transpose(banks[c][:, t, :], g[c // 2][:, (c % 2) * P:(c % 2 + 1) * P], ident[:])
            for h in range(2):
                nc.vector.tensor_scalar(gd[h][:, t, :], g[h][:], dsc_col[:, t:t + 1], None, op0=ALU.mult)
            for c in range(CHUNKS):
                nc.scalar.activation(junk[:, t, c, :], banks[c][:, t, :], ACT.Square, scale=root, accum_out=ms[t][c][:])
                if t > 0:
                    nc.scalar.activation(run[t][c][:], ms[t][c][:], ACT.Sqrt if t == last else ACT.Identity, bias=run[t - 1][c][:])
        rms = run[last]
        nc.scalar.activation(warm[:], rms[CHUNKS - 1][:], ACT.Exp, scale=-1.0)

        q_bf = [sb.tile([P, P * PACK], BF16, name=f"q_bf{j}", align_bytes=64) for j in range(2)]
        q_codes = [sb.tile([P, P], U32, name=f"q_codes{j}", align_bytes=64) for j in range(2)]
        q_scales = [sb.tile([P, P], U8, name=f"q_scales{j}", align_bytes=64) for j in range(2)]
        for c in range(CHUNKS):
            nc.vector.reciprocal(inv[c][:], rms[c][:])
            j, u = c // 2, c % 2
            nc.vector.tensor_copy(q_bf[j][:, u * 256:(u + 1) * 256].rearrange("p (c i t) -> p c t i", i=4, t=PACK),
                                  q_raw[:, :, c * 64:(c + 1) * 64].rearrange("p t (c i) -> p c t i", i=4))
            nc.vector.tensor_scalar(fac[c][:], inv[c][:], lim_col[:, c:c + 1], 1.0, op0=ALU.mult, op1=ALU.min)
            nc.tensor.transpose(banks[c][:, 0, :], fac[c][:].to_broadcast([P, P]), ident[:])

        km = [sb.tile([P, P * PACK], BF16, name=f"km{c}", align_bytes=64) for c in range(CHUNKS)]
        k_codes = [sb.tile([P, P], U32, name=f"k_codes{c}", align_bytes=64) for c in range(CHUNKS)]
        k_scales = [sb.tile([P, P], U8, name=f"k_scales{c}", align_bytes=64) for c in range(CHUNKS)]

        def scale_keys(c):
            h, cols = c // 2, slice((c % 2) * P, (c % 2 + 1) * P)
            nc.vector.tensor_tensor(
                km[c][:].rearrange("p (c i t) -> p c t i", i=4, t=PACK),
                banks[c][:, 0, :].rearrange("p (c o i) -> p c o i", o=1, i=4).to_broadcast([P, P // 4, PACK, 4]),
                gd[h][:, :, cols].rearrange("p t (c i) -> p c t i", i=4),
                ALU.mult,
            )

        def score(c):
            nc.vector.quantize_mx(out=k_codes[c][:].bitcast(FP8X4), scales=k_scales[c][:], in_=km[c][:])
            for j in range(2):
                target = first[j][:, c, :] if c < 2 else second[j][:, c, :]
                nc.tensor.matmul_mx(
                    out=target,
                    lhsT=q_codes[j][:].bitcast(FP8X4),
                    lhsT_scale=q_scales[j][:],
                    rhs=k_codes[c][:].bitcast(FP8X4),
                    rhs_scale=k_scales[c][:],
                    start=True,
                    stop=True,
                )

        neg_first = [sb.tile([P, 1], F32, name=f"neg_first{j}") for j in range(2)]
        neg_max = [sb.tile([P, 1], F32, name=f"neg_max{j}") for j in range(2)]
        sum_first = [sb.tile([P, 1], F32, name=f"sum_first{j}") for j in range(2)]
        sum_second = [sb.tile([P, 1], F32, name=f"sum_second{j}") for j in range(2)]
        shift = [sb.tile([P, 1], F32, name=f"shift{j}") for j in range(2)]
        part = [sb.tile([P, 1], F32, name=f"part{j}") for j in range(2)]
        total = [sb.tile([P, 1], F32, name=f"total{j}") for j in range(2)]
        norm = [sb.tile([P, 1], F32, name=f"norm{j}") for j in range(2)]
        e = [[sb.tile([P, HALF], F32, name=f"e{j}_{h}") for h in range(2)] for j in range(2)]
        y = [sb.tile([P, I], F32, name=f"y{j}") for j in range(2)]
        negated = sb.tile([P, 2, HALF], F32, name="negated")

        for j in range(2):
            nc.vector.quantize_mx(out=q_codes[j][:].bitcast(FP8X4), scales=q_scales[j][:], in_=q_bf[j][:])
        scale_keys(0)
        scale_keys(1)
        score(0)
        scale_keys(2)
        score(1)
        scale_keys(3)
        score(2)
        for j in range(2):
            a = first[j][:, 0:2, :].rearrange("p c s -> p (c s)")
            nc.vector.tensor_reduce(neg_first[j][:], a, AX.X, ALU.max, negate=True)
            nc.scalar.activation(e[j][0][:], a, ACT.Exp, bias=neg_first[j][:], accum_out=sum_first[j][:])
            if j == 0:
                score(3)
        for j in range(2):
            a = second[j][:, 2:4, :].rearrange("p c s -> p (c s)")
            nc.vector.tensor_scalar(negated[:, j, :], a, -1.0, neg_first[j][:], op0=ALU.mult, op1=ALU.min, accum_out=neg_max[j][:])
            nc.scalar.activation(shift[j][:], neg_first[j][:], ACT.Exp, bias=neg_max[j][:], scale=-1.0)
            nc.scalar.activation(e[j][1][:], a, ACT.Exp, bias=neg_max[j][:], accum_out=sum_second[j][:])
        for j in range(2):
            nc.vector.tensor_scalar(part[j][:], sum_first[j][:], shift[j][:], 1.0 / I, op0=ALU.mult, op1=ALU.mult)
        for j in range(2):
            nc.vector.tensor_scalar(total[j][:], sum_second[j][:], 1.0 / I, part[j][:], op0=ALU.mult, op1=ALU.add)
            if j == 1:
                nc.vector.tensor_scalar(y[0][:, 0:HALF], e[0][0][:], shift[0][:], norm[0][:], op0=ALU.mult, op1=ALU.mult)
            nc.vector.reciprocal(norm[j][:], total[j][:])
        nc.scalar.activation(y[0][:, HALF:I], e[0][1][:], ACT.Copy, scale=norm[0][:])
        nc.sync.dma_start(out[0:P, :], y[0][:])
        nc.vector.tensor_scalar(y[1][:, 0:HALF], e[1][0][:], shift[1][:], norm[1][:], op0=ALU.mult, op1=ALU.mult)
        nc.scalar.activation(y[1][:, HALF:I], e[1][1][:], ACT.Copy, scale=norm[1][:])
        nc.sync.dma_start(out[P:2 * P, :], y[1][:])
